import numpy as np
import ml_dtypes


def mxq(x, axis, fmt="e4m3"):
    dtype, down = {"e4m3": (ml_dtypes.float8_e4m3fn, 7), "e5m2": (ml_dtypes.float8_e5m2, 14)}[fmt]
    v = np.moveaxis(np.asarray(x, np.float32).astype(ml_dtypes.bfloat16).astype(np.float64), axis, -1)
    blocks = v.reshape(v.shape[:-1] + (-1, 32))
    amax = np.abs(blocks).max(-1, keepdims=True)
    byte = np.maximum(np.where(amax > 0, np.frexp(amax)[1] - 1 + 127, 0) - down, 1)
    scale = np.exp2(byte - 127.0)
    codes = (blocks / scale).astype(np.float32).astype(dtype).astype(np.float64)
    return np.moveaxis((codes * scale).reshape(v.shape), -1, axis)


WIDE = False


def mx_kscale(k):
    if not WIDE:
        return np.ones(k)
    levels = np.array([10, -10, 5, -5, 0])
    if k % 512:
        return np.exp2(np.random.permutation(np.resize(levels, k // 32))).repeat(32)
    a = np.empty((k // 512, 16))
    for p in range(k // 512):
        a[p, :8] = np.random.permutation(np.resize(levels, 8))
        for g in range(8):
            far = levels[np.abs(levels - a[p, g]) >= 10]
            a[p, g + 8] = far[np.random.randint(len(far))]
    return np.exp2(a.ravel()).repeat(32)


def f64(x):
    return np.asarray(x).astype(np.float64)


def striped8(idx):
    return np.concatenate([v.reshape(-1, 16).T for v in idx]).astype(np.uint16)


def unstriped8(offs):
    return np.stack([offs[16 * g:16 * g + 16].T.reshape(-1) for g in range(8)]).astype(np.int64)


E2M1 = np.array([0.0, 0.5, 1.0, 1.5, 2.0, 3.0, 4.0, 6.0, -0.0, -0.5, -1.0, -1.5, -2.0, -3.0, -4.0, -6.0])


def pack_weight(w, fmt):
    k, n = w.shape
    w = f64(np.asarray(w, np.float32).astype(ml_dtypes.bfloat16)).reshape(k // 32, 32, n)
    amax = np.abs(w).max(1)
    if fmt == "e4m3":
        byte = np.frexp(amax)[1] - 1 + 127 - 7
    else:
        mant, ex = np.frexp(amax / 6.0)
        byte = np.where(mant > 0.5, ex, ex - 1) + 127
    byte = np.clip(np.where(amax > 0, byte, 1), 1, 254)
    scaled = (w * np.exp2(127.0 - byte)[:, None, :]).reshape(k, n).astype(np.float32)
    by_word = np.ascontiguousarray(scaled.reshape(k // 512, 128, 4, n).transpose(0, 1, 3, 2))
    if fmt == "e4m3":
        words = by_word.astype(ml_dtypes.float8_e4m3fn).view(np.uint8)
    else:
        c = by_word.astype(ml_dtypes.float4_e2m1fn).view(np.uint8) & 0xF
        words = (c[..., 0::2] | (c[..., 1::2] << 4)).reshape(k // 512, 128, 2 * n)
    return np.ascontiguousarray(words), np.ascontiguousarray(byte.astype(np.uint8).reshape(k // 512, 16, n))


def unpack_weight(words, scales, fmt):
    g, _, n = scales.shape
    words = np.ascontiguousarray(words).reshape(g, 128, n, -1)
    if fmt == "e4m3":
        vals = words.view(ml_dtypes.float8_e4m3fn).astype(np.float64)
    else:
        nib = np.empty((g, 128, n, 4), np.uint8)
        nib[..., 0::2] = words & 0xF
        nib[..., 1::2] = words >> 4
        vals = E2M1[nib]
    vals = vals * np.repeat(np.exp2(scales.astype(np.float64) - 127.0), 8, axis=1)[..., None]
    return vals.transpose(0, 1, 3, 2).reshape(g * 512, n)


def silu(v):
    return v / (1.0 + np.exp(-np.maximum(v, -700.0)))


K, M, T, S = 512, 256, 4096, 2048


def setup_inputs():
    n = np.random.standard_normal
    s = mx_kscale(K)[:, None]
    u = mx_kscale(512)[:, None]
    p_w2 = pack_weight(1.4 * n((512, M)) / np.sqrt(512) / u, "e2m1")
    return {
        "x": (n((K, S)) * s).astype(np.float32),
        "w1": (n((K, 512)) / np.sqrt(K) / s * u.T).astype(np.float32),
        "w2_words": p_w2[0],
        "w2_scales": p_w2[1],
        "b": (0.3 * n(256)).astype(np.float32),
        "wgo": np.repeat(np.random.uniform(0.5, 2.0, (8, S)), 16, axis=0).astype(np.float32),
        "offs": striped8(np.stack([np.random.permutation(T)[:S] for _ in range(8)])),
    }


def reference(x, w1, w2_words, w2_scales, b, wgo, offs):
    x_ = mxq(f64(x), 0, "e4m3")
    w1_ = mxq(f64(w1), 0, "e4m3")
    w2_ = unpack_weight(w2_words, w2_scales, "e2m1")
    h_ = mxq(np.maximum(w1_.T @ x_, 0.0), 0, "e4m3")
    y = w2_.T @ h_
    place = unstriped8(offs)[np.arange(M) % 128 // 16]
    out = np.zeros((M, T))
    out[np.arange(M)[:, None], place] = f64(wgo)[np.arange(M) % 128] * (silu(y + f64(b)[:, None]))
    return out

@@ -1,0 +1,204 @@
+from contextlib import ExitStack
+
+import concourse.mybir as mybir
+
+K, H, M, T, S = 512, 512, 256, 4096, 2048
+FLOPS = 2 * K * H * S + 2 * H * M * S
+
+F32 = mybir.dt.float32
+BF16 = mybir.dt.bfloat16
+I32 = mybir.dt.int32
+U32 = mybir.dt.uint32
+U16 = mybir.dt.uint16
+U8 = mybir.dt.uint8
+FP8X4 = mybir.dt.float8_e4m3fn_x4
+FP4X4 = mybir.dt.float4_e2m1fn_x4
+ACT = mybir.ActivationFunctionType
+ALU = mybir.AluOpType
+
+P = 128
+PACK = 4
+CH = 256
+NCH = S // CH
+BANK_COLS = 128
+H_BANKS = 6
+Y_BANKS = 2
+
+
+def tile_list_hscat_m_silu_kernel(tc, x, w1, w2_words, w2_scales, b, wgo, offs, out):
+    nc = tc.nc
+    with ExitStack() as ctx:
+        keep = ctx.enter_context(tc.tile_pool(name="keep", bufs=1))
+        psum = ctx.enter_context(tc.psum_pool(name="psum", bufs=1))
+
+        offsets = keep.tile([P, S // 16], U16, name="offsets")
+        pages = [keep.tile([P, T], F32, name="page%d" % h) for h in range(2)]
+        gated = [keep.tile([P, S], F32, name="gated%d" % h) for h in range(2)]
+        wgo_sb = keep.tile([P, S], F32, name="wgo_sb")
+        bias = keep.tile([P, 2], F32, name="bias")
+        zero = keep.tile([P, 1], F32, name="zero")
+        relu_bias = keep.tile([P, 1], F32, name="relu_bias")
+        w1_raw = [keep.tile([P, PACK, H // 2], F32, name="w1_raw%d" % u) for u in range(2)]
+        w1_bf = keep.tile([P, PACK * H], BF16, name="w1_bf", align_bytes=64)
+        w1_codes = keep.tile([P, H], U32, name="w1_codes", align_bytes=64)
+        w1_scales = keep.tile([P, H], U8, name="w1_scales", align_bytes=64)
+        w2_codes = keep.tile([P, 2 * M], U8, name="w2_codes", align_bytes=64)
+        w2_plane = keep.tile([P, M], U8, name="w2_plane", align_bytes=64)
+        x_raw = [keep.tile([P, PACK, CH], F32, name="x_raw%d" % c) for c in range(NCH)]
+        x_bf = [keep.tile([P, PACK * CH], BF16, name="x_bf%d" % c, align_bytes=64) for c in range(NCH)]
+        x_codes = [keep.tile([P, CH], U32, name="x_codes%d" % c, align_bytes=64) for c in range(NCH)]
+        x_scales = [keep.tile([P, CH], U8, name="x_scales%d" % c, align_bytes=64) for c in range(NCH)]
+        h_bf = [keep.tile([P, PACK * CH], BF16, name="h_bf%d" % c, align_bytes=64) for c in range(NCH)]
+        h_codes = [keep.tile([P, CH], U32, name="h_codes%d" % c, align_bytes=64) for c in range(NCH)]
+        h_scales = [keep.tile([P, CH], U8, name="h_scales%d" % c, align_bytes=64) for c in range(NCH)]
+        h_banks = [psum.tile([P, PACK, BANK_COLS], F32, name="h_bank%d" % i) for i in range(H_BANKS)]
+        y_banks = [psum.tile([P, CH], F32, name="y_bank%d" % i) for i in range(Y_BANKS)]
+
+        x_view = x.rearrange("(p j) s -> p j s", j=PACK)
+        w1_view = w1.rearrange("(p j) r -> p j r", j=PACK)
+
+        def load_x(c):
+            nc.sync.dma_start(out=x_raw[c][:], in_=x_view[:, :, c * CH : (c + 1) * CH])
+
+        def load_wgo(a, z):
+            nc.sync.dma_start(out=wgo_sb[:, a:z], in_=wgo[:, a:z])
+
+        nc.gpsimd.memset(zero[:], 0.0)
+        nc.gpsimd.memset(w2_plane[:].bitcast(I32), 0)
+        nc.scalar.activation(out=relu_bias[:], in_=zero[:], func=ACT.Silu)
+
+        nc.sync.dma_start(out=w1_raw[0][:], in_=w1_view[:, :, 0 : H // 2])
+        load_x(0)
+        nc.sync.dma_start(out=w1_raw[1][:], in_=w1_view[:, :, H // 2 : H])
+        load_x(1)
+        for q in range(4):
+            nc.sync.dma_start(
+                out=w2_plane[32 * q : 32 * q + 4, :].bitcast(I32),
+                in_=w2_scales[0, 4 * q : 4 * q + 4, :].bitcast(I32),
+            )
+        nc.sync.dma_start(out=w2_codes[:].bitcast(I32), in_=w2_words[0].bitcast(I32))
+        with nc.allow_non_contiguous_dma(reason="one bias value to a partition"):
+            nc.sync.dma_start(out=bias[:], in_=b.rearrange("(h p) -> p h", p=P))
+        nc.sync.dma_start(offsets[:], offs)
+        load_wgo(0, 512)
+        load_x(2)
+        load_x(3)
+        load_wgo(512, 1024)
+        load_x(4)
+        load_x(5)
+        load_wgo(1024, 2048)
+        load_x(6)
+        load_x(7)
+
+        nc.vector.memset(pages[0][:, 0:2047], 0.0)
+        nc.vector.memset(pages[0][:, 2047:T], 0.0)
+        nc.gpsimd.memset(pages[1][:], 0.0)
+
+        def cast(on_vector, dst, src):
+            if on_vector:
+                nc.vector.tensor_copy(out=dst, in_=src)
+            else:
+                nc.scalar.copy(out=dst, in_=src)
+
+        def cast_w1(u, on_vector):
+            dst = w1_bf[:].rearrange("p (t m j) -> p m j t", t=PACK, j=PACK)[:, 64 * u : 64 * (u + 1)]
+            cast(on_vector, dst, w1_raw[u][:].rearrange("p j (m t) -> p m j t", t=PACK))
+
+        def cast_x(c, on_vector):
+            dst = x_bf[c][:].rearrange("p (g i j) -> p g j i", i=4, j=PACK)
+            cast(on_vector, dst, x_raw[c][:].rearrange("p j (g i) -> p g j i", i=4))
+
+        def quant_x(c):
+            nc.vector.quantize_mx(out=x_codes[c][:].bitcast(FP8X4), scales=x_scales[c][:], in_=x_bf[c][:])
+
+        def first_layer(c, vector_blocks):
+            for i in range(CH // BANK_COLS):
+                bank = h_banks[(c * (CH // BANK_COLS) + i) % H_BANKS]
+                cols = slice(i * BANK_COLS, (i + 1) * BANK_COLS)
+                for t in range(PACK):
+                    nc.tensor.matmul_mx(
+                        out=bank[:, t, :],
+                        lhsT=w1_codes[:, t * P : (t + 1) * P].bitcast(FP8X4),
+                        lhsT_scale=w1_scales[:, t * P : (t + 1) * P],
+                        rhs=x_codes[c][:, cols].bitcast(FP8X4),
+                        rhs_scale=x_scales[c][:, cols],
+                        start=True,
+                        stop=True,
+                    )
+                dst = h_bf[c][:, i * PACK * BANK_COLS : (i + 1) * PACK * BANK_COLS].rearrange("p (n t) -> p n t", t=PACK)
+                src = bank[:].rearrange("p t n -> p n t")
+                if i in vector_blocks:
+                    nc.vector.tensor_scalar(out=dst, in0=src, scalar1=0.0, scalar2=None, op0=ALU.max)
+                else:
+                    nc.scalar.activation(out=dst, in_=src, func=ACT.Relu, bias=relu_bias[:])
+            nc.vector.quantize_mx(out=h_codes[c][:].bitcast(FP8X4), scales=h_scales[c][:], in_=h_bf[c][:])
+
+        uses = []
+
+        def second_layer(h, c):
+            bank = y_banks[len(uses) % Y_BANKS]
+            uses.append((h, c))
+            nc.tensor.matmul_mx(
+                out=bank[:],
+                lhsT=w2_codes[:, 2 * P * h : 2 * P * (h + 1)].bitcast(FP4X4),
+                lhsT_scale=w2_plane[:, P * h : P * (h + 1)],
+                rhs=h_codes[c][:].bitcast(FP8X4),
+                rhs_scale=h_scales[c][:],
+                start=True,
+                stop=True,
+            )
+            nc.scalar.activation(
+                out=gated[h][:, c * CH : (c + 1) * CH], in_=bank[:], func=ACT.Silu, bias=bias[:, h : h + 1]
+            )
+
+        def place(h, c0, c1):
+            for c in range(c0, c1):
+                second_layer(h, c)
+            a, z = c0 * CH, c1 * CH
+            nc.vector.tensor_tensor(
+                pages[h][:].indirect(offsets[:, a // 16 : z // 16]), gated[h][:, a:z], wgo_sb[:, a:z], ALU.mult
+            )
+
+        def store(h):
+            for a in range(0, T, 2048):
+                nc.sync.dma_start(out=out[h * P : (h + 1) * P, a : a + 2048], in_=pages[h][:, a : a + 2048])
+
+        def prepare(c):
+            cast_x(c, False)
+            quant_x(c)
+
+        cast_w1(0, False)
+        cast_x(0, False)
+        quant_x(0)
+        cast_w1(1, True)
+        nc.vector.quantize_mx(out=w1_codes[:].bitcast(FP8X4), scales=w1_scales[:], in_=w1_bf[:])
+        prepare(1)
+        first_layer(0, (1,))
+        place(0, 0, 1)
+        first_layer(1, (0,))
+        place(1, 0, 1)
+        prepare(2)
+        place(0, 1, 2)
+        prepare(3)
+        first_layer(2, ())
+        place(1, 1, 2)
+        prepare(4)
+        first_layer(3, ())
+        place(0, 2, 3)
+        prepare(5)
+        first_layer(4, ())
+        place(1, 2, 3)
+        place(0, 3, 4)
+        prepare(6)
+        first_layer(5, ())
+        place(1, 3, 4)
+        place(0, 4, 5)
+        prepare(7)
+        first_layer(6, ())
+        place(1, 4, 5)
+        place(0, 5, 6)
+        first_layer(7, ())
+        place(0, 6, 8)
+        store(0)
+        place(1, 5, 8)
+        store(1)

@@ -20,9 +20,8 @@ P = 128
 PACK = 4
 CH = 256
 NCH = S // CH
-BANK_COLS = 128
+BLOCK = 128
 H_BANKS = 6
-Y_BANKS = 2
 
 
 def tile_list_hscat_m_silu_kernel(tc, x, w1, w2_words, w2_scales, b, wgo, offs, out):
@@ -45,14 +44,13 @@ def tile_list_hscat_m_silu_kernel(tc, x, w1, w2_words, w2_scales, b, wgo, offs, 
         w2_codes = keep.tile([P, 2 * M], U8, name="w2_codes", align_bytes=64)
         w2_plane = keep.tile([P, M], U8, name="w2_plane", align_bytes=64)
         x_raw = [keep.tile([P, PACK, CH], F32, name="x_raw%d" % c) for c in range(NCH)]
-        x_bf = [keep.tile([P, PACK * CH], BF16, name="x_bf%d" % c, align_bytes=64) for c in range(NCH)]
-        x_codes = [keep.tile([P, CH], U32, name="x_codes%d" % c, align_bytes=64) for c in range(NCH)]
-        x_scales = [keep.tile([P, CH], U8, name="x_scales%d" % c, align_bytes=64) for c in range(NCH)]
-        h_bf = [keep.tile([P, PACK * CH], BF16, name="h_bf%d" % c, align_bytes=64) for c in range(NCH)]
-        h_codes = [keep.tile([P, CH], U32, name="h_codes%d" % c, align_bytes=64) for c in range(NCH)]
-        h_scales = [keep.tile([P, CH], U8, name="h_scales%d" % c, align_bytes=64) for c in range(NCH)]
-        h_banks = [psum.tile([P, PACK, BANK_COLS], F32, name="h_bank%d" % i) for i in range(H_BANKS)]
-        y_banks = [psum.tile([P, CH], F32, name="y_bank%d" % i) for i in range(Y_BANKS)]
+        x_bf = keep.tile([P, PACK * S], BF16, name="x_bf", align_bytes=64)
+        x_codes = keep.tile([P, S], U32, name="x_codes", align_bytes=64)
+        x_scales = keep.tile([P, S], U8, name="x_scales", align_bytes=64)
+        h_bf = keep.tile([P, PACK * S], BF16, name="h_bf", align_bytes=64)
+        h_codes = keep.tile([P, S], U32, name="h_codes", align_bytes=64)
+        h_scales = keep.tile([P, S], U8, name="h_scales", align_bytes=64)
+        banks = [psum.tile([P, PACK * BLOCK], F32, name="bank%d" % i) for i in range(8)]
 
         x_view = x.rearrange("(p j) s -> p j s", j=PACK)
         w1_view = w1.rearrange("(p j) r -> p j r", j=PACK)
@@ -63,31 +61,31 @@ def tile_list_hscat_m_silu_kernel(tc, x, w1, w2_words, w2_scales, b, wgo, offs, 
         def load_wgo(a, z):
             nc.sync.dma_start(out=wgo_sb[:, a:z], in_=wgo[:, a:z])
 
-        nc.gpsimd.memset(zero[:], 0.0)
         nc.gpsimd.memset(w2_plane[:].bitcast(I32), 0)
-        nc.scalar.activation(out=relu_bias[:], in_=zero[:], func=ACT.Silu)
-
-        nc.sync.dma_start(out=w1_raw[0][:], in_=w1_view[:, :, 0 : H // 2])
-        load_x(0)
-        nc.sync.dma_start(out=w1_raw[1][:], in_=w1_view[:, :, H // 2 : H])
-        load_x(1)
+        nc.gpsimd.memset(zero[:], 0.0)
         for q in range(4):
-            nc.sync.dma_start(
+            nc.scalar.dma_start(
                 out=w2_plane[32 * q : 32 * q + 4, :].bitcast(I32),
                 in_=w2_scales[0, 4 * q : 4 * q + 4, :].bitcast(I32),
             )
-        nc.sync.dma_start(out=w2_codes[:].bitcast(I32), in_=w2_words[0].bitcast(I32))
         with nc.allow_non_contiguous_dma(reason="one bias value to a partition"):
-            nc.sync.dma_start(out=bias[:], in_=b.rearrange("(h p) -> p h", p=P))
+            nc.scalar.dma_start(out=bias[:], in_=b.rearrange("(h p) -> p h", p=P))
+        nc.scalar.activation(out=relu_bias[:], in_=zero[:], func=ACT.Silu)
+
+        nc.sync.dma_start(out=w1_raw[0][:], in_=w1_view[:, :, 0 : H // 2])
+        nc.sync.dma_start(out=w1_raw[1][:], in_=w1_view[:, :, H // 2 : H])
+        load_x(0)
+        nc.sync.dma_start(out=w2_codes[:].bitcast(I32), in_=w2_words[0].bitcast(I32))
+        load_x(1)
+        load_x(2)
         nc.sync.dma_start(offsets[:], offs)
         load_wgo(0, 512)
-        load_x(2)
         load_x(3)
-        load_wgo(512, 1024)
         load_x(4)
+        load_wgo(512, 1024)
         load_x(5)
-        load_wgo(1024, 2048)
         load_x(6)
+        load_wgo(1024, 2048)
         load_x(7)
 
         nc.vector.memset(pages[0][:, 0:2047], 0.0)
@@ -104,101 +102,100 @@ def tile_list_hscat_m_silu_kernel(tc, x, w1, w2_words, w2_scales, b, wgo, offs, 
             dst = w1_bf[:].rearrange("p (t m j) -> p m j t", t=PACK, j=PACK)[:, 64 * u : 64 * (u + 1)]
             cast(on_vector, dst, w1_raw[u][:].rearrange("p j (m t) -> p m j t", t=PACK))
 
-        def cast_x(c, on_vector):
-            dst = x_bf[c][:].rearrange("p (g i j) -> p g j i", i=4, j=PACK)
-            cast(on_vector, dst, x_raw[c][:].rearrange("p j (g i) -> p g j i", i=4))
+        def cast_x(a, z, on_vector):
+            c = a // CH
+            dst = x_bf[:, PACK * a : PACK * z].rearrange("p (g i j) -> p g j i", i=4, j=PACK)
+            cast(on_vector, dst, x_raw[c][:, :, a - c * CH : z - c * CH].rearrange("p j (g i) -> p g j i", i=4))
 
-        def quant_x(c):
-            nc.vector.quantize_mx(out=x_codes[c][:].bitcast(FP8X4), scales=x_scales[c][:], in_=x_bf[c][:])
+        def quant_x(a, z):
+            nc.vector.quantize_mx(
+                out=x_codes[:, a:z].bitcast(FP8X4), scales=x_scales[:, a:z], in_=x_bf[:, PACK * a : PACK * z]
+            )
 
-        def first_layer(c, vector_blocks):
-            for i in range(CH // BANK_COLS):
-                bank = h_banks[(c * (CH // BANK_COLS) + i) % H_BANKS]
-                cols = slice(i * BANK_COLS, (i + 1) * BANK_COLS)
+        def quant_h(a, z):
+            nc.vector.quantize_mx(
+                out=h_codes[:, a:z].bitcast(FP8X4), scales=h_scales[:, a:z], in_=h_bf[:, PACK * a : PACK * z]
+            )
+
+        def first_layer(c):
+            for a in range(c * CH, (c + 1) * CH, BLOCK):
+                bank = banks[a // BLOCK % H_BANKS]
                 for t in range(PACK):
                     nc.tensor.matmul_mx(
-                        out=bank[:, t, :],
+                        out=bank[:, t * BLOCK : (t + 1) * BLOCK],
                         lhsT=w1_codes[:, t * P : (t + 1) * P].bitcast(FP8X4),
                         lhsT_scale=w1_scales[:, t * P : (t + 1) * P],
-                        rhs=x_codes[c][:, cols].bitcast(FP8X4),
-                        rhs_scale=x_scales[c][:, cols],
+                        rhs=x_codes[:, a : a + BLOCK].bitcast(FP8X4),
+                        rhs_scale=x_scales[:, a : a + BLOCK],
                         start=True,
                         stop=True,
                     )
-                dst = h_bf[c][:, i * PACK * BANK_COLS : (i + 1) * PACK * BANK_COLS].rearrange("p (n t) -> p n t", t=PACK)
-                src = bank[:].rearrange("p t n -> p n t")
-                if i in vector_blocks:
-                    nc.vector.tensor_scalar(out=dst, in0=src, scalar1=0.0, scalar2=None, op0=ALU.max)
-                else:
-                    nc.scalar.activation(out=dst, in_=src, func=ACT.Relu, bias=relu_bias[:])
-            nc.vector.quantize_mx(out=h_codes[c][:].bitcast(FP8X4), scales=h_scales[c][:], in_=h_bf[c][:])
+                nc.scalar.activation(
+                    out=h_bf[:, PACK * a : PACK * (a + BLOCK)].rearrange("p (n t) -> p n t", t=PACK),
+                    in_=bank[:].rearrange("p (t n) -> p n t", t=PACK),
+                    func=ACT.Relu,
+                    bias=relu_bias[:],
+                )
 
-        uses = []
-
-        def second_layer(h, c):
-            bank = y_banks[len(uses) % Y_BANKS]
-            uses.append((h, c))
+        def second_layer(h, a, z, bank, dst):
             nc.tensor.matmul_mx(
-                out=bank[:],
+                out=bank[:, 0 : z - a],
                 lhsT=w2_codes[:, 2 * P * h : 2 * P * (h + 1)].bitcast(FP4X4),
                 lhsT_scale=w2_plane[:, P * h : P * (h + 1)],
-                rhs=h_codes[c][:].bitcast(FP8X4),
-                rhs_scale=h_scales[c][:],
+                rhs=h_codes[:, a:z].bitcast(FP8X4),
+                rhs_scale=h_scales[:, a:z],
                 start=True,
                 stop=True,
             )
-            nc.scalar.activation(
-                out=gated[h][:, c * CH : (c + 1) * CH], in_=bank[:], func=ACT.Silu, bias=bias[:, h : h + 1]
-            )
+            nc.scalar.activation(out=dst, in_=bank[:, 0 : z - a], func=ACT.Silu, bias=bias[:, h : h + 1])
 
-        def place(h, c0, c1):
-            for c in range(c0, c1):
-                second_layer(h, c)
-            a, z = c0 * CH, c1 * CH
-            nc.vector.tensor_tensor(
-                pages[h][:].indirect(offsets[:, a // 16 : z // 16]), gated[h][:, a:z], wgo_sb[:, a:z], ALU.mult
-            )
+        def scatter(h, a, z, src):
+            nc.vector.tensor_tensor(pages[h][:].indirect(offsets[:, a // 16 : z // 16]), src, wgo_sb[:, a:z], ALU.mult)
 
         def store(h):
             for a in range(0, T, 2048):
                 nc.sync.dma_start(out=out[h * P : (h + 1) * P, a : a + 2048], in_=pages[h][:, a : a + 2048])
 
-        def prepare(c):
-            cast_x(c, False)
-            quant_x(c)
-
         cast_w1(0, False)
-        cast_x(0, False)
-        quant_x(0)
         cast_w1(1, True)
         nc.vector.quantize_mx(out=w1_codes[:].bitcast(FP8X4), scales=w1_scales[:], in_=w1_bf[:])
-        prepare(1)
-        first_layer(0, (1,))
-        place(0, 0, 1)
-        first_layer(1, (0,))
-        place(1, 0, 1)
-        prepare(2)
-        place(0, 1, 2)
-        prepare(3)
-        first_layer(2, ())
-        place(1, 1, 2)
-        prepare(4)
-        first_layer(3, ())
-        place(0, 2, 3)
-        prepare(5)
-        first_layer(4, ())
-        place(1, 2, 3)
-        place(0, 3, 4)
-        prepare(6)
-        first_layer(5, ())
-        place(1, 3, 4)
-        place(0, 4, 5)
-        prepare(7)
-        first_layer(6, ())
-        place(1, 4, 5)
-        place(0, 5, 6)
-        first_layer(7, ())
-        place(0, 6, 8)
+        for a in (0, BLOCK):
+            cast_x(a, a + BLOCK, False)
+            quant_x(a, a + BLOCK)
+        first_layer(0)
+        quant_h(0, CH)
+        cast_x(CH, 2 * CH, True)
+        quant_x(CH, 2 * CH)
+        second_layer(0, 0, CH, banks[6], gated[0][:, 0:CH])
+        cast_x(2 * CH, 3 * CH, True)
+        quant_x(2 * CH, 3 * CH)
+        scatter(0, 0, CH, gated[0][:, 0:CH])
+        first_layer(1)
+        second_layer(1, 0, CH, banks[7], gated[1][:, 0:CH])
+        quant_h(CH, 2 * CH)
+        scatter(1, 0, CH, gated[1][:, 0:CH])
+        for k in range(1, 5):
+            ahead = range(k + 2, k + 3) if k < 4 else range(6, 8)
+            for c in ahead:
+                cast_x(c * CH, (c + 1) * CH, False)
+            first_layer(k + 1)
+            quant_h((k + 1) * CH, (k + 2) * CH)
+            quant_x(ahead.start * CH, ahead.stop * CH)
+            spent = x_raw[ahead.stop - 1]
+            for h in range(2):
+                second_layer(h, k * CH, (k + 1) * CH, banks[6 + h], spent[:, h, :])
+            for h in range(2):
+                scatter(h, k * CH, (k + 1) * CH, spent[:, h, :])
+        first_layer(6)
+        first_layer(7)
+        quant_h(6 * CH, 8 * CH)
+        last = banks[15 % H_BANKS]
+        second_layer(0, 5 * CH, 6 * CH, last, gated[0][:, 5 * CH : 6 * CH])
+        scatter(0, 5 * CH, 6 * CH, gated[0][:, 5 * CH : 6 * CH])
+        second_layer(0, 6 * CH, S, banks[6], gated[0][:, 6 * CH : S])
+        second_layer(1, 5 * CH, 6 * CH, last, gated[1][:, 5 * CH : 6 * CH])
+        second_layer(1, 6 * CH, S, banks[7], gated[1][:, 6 * CH : S])
+        scatter(0, 6 * CH, S, gated[0][:, 6 * CH : S])
         store(0)
-        place(1, 5, 8)
+        scatter(1, 5 * CH, S, gated[1][:, 5 * CH : S])
         store(1)

@@ -37,7 +37,7 @@ def tile_list_hscat_m_silu_kernel(tc, x, w1, w2_words, w2_scales, b, wgo, offs, 
         bias = keep.tile([P, 2], F32, name="bias")
         zero = keep.tile([P, 1], F32, name="zero")
         relu_bias = keep.tile([P, 1], F32, name="relu_bias")
-        w1_raw = [keep.tile([P, PACK, H // 2], F32, name="w1_raw%d" % u) for u in range(2)]
+        w1_raw = keep.tile([P, PACK, H], F32, name="w1_raw")
         w1_bf = keep.tile([P, PACK * H], BF16, name="w1_bf", align_bytes=64)
         w1_codes = keep.tile([P, H], U32, name="w1_codes", align_bytes=64)
         w1_scales = keep.tile([P, H], U8, name="w1_scales", align_bytes=64)
@@ -68,16 +68,15 @@ def tile_list_hscat_m_silu_kernel(tc, x, w1, w2_words, w2_scales, b, wgo, offs, 
                 out=w2_plane[32 * q : 32 * q + 4, :].bitcast(I32),
                 in_=w2_scales[0, 4 * q : 4 * q + 4, :].bitcast(I32),
             )
-        with nc.allow_non_contiguous_dma(reason="one bias value to a partition"):
-            nc.scalar.dma_start(out=bias[:], in_=b.rearrange("(h p) -> p h", p=P))
         nc.scalar.activation(out=relu_bias[:], in_=zero[:], func=ACT.Silu)
 
-        nc.sync.dma_start(out=w1_raw[0][:], in_=w1_view[:, :, 0 : H // 2])
-        nc.sync.dma_start(out=w1_raw[1][:], in_=w1_view[:, :, H // 2 : H])
+        nc.sync.dma_start(out=w1_raw[:], in_=w1_view)
         load_x(0)
-        nc.sync.dma_start(out=w2_codes[:].bitcast(I32), in_=w2_words[0].bitcast(I32))
         load_x(1)
+        nc.sync.dma_start(out=w2_codes[:].bitcast(I32), in_=w2_words[0].bitcast(I32))
         load_x(2)
+        with nc.allow_non_contiguous_dma(reason="one bias value to a partition"):
+            nc.sync.dma_start(out=bias[:], in_=b.rearrange("(h p) -> p h", p=P))
         nc.sync.dma_start(offsets[:], offs)
         load_wgo(0, 512)
         load_x(3)
@@ -98,9 +97,9 @@ def tile_list_hscat_m_silu_kernel(tc, x, w1, w2_words, w2_scales, b, wgo, offs, 
             else:
                 nc.scalar.copy(out=dst, in_=src)
 
-        def cast_w1(u, on_vector):
-            dst = w1_bf[:].rearrange("p (t m j) -> p m j t", t=PACK, j=PACK)[:, 64 * u : 64 * (u + 1)]
-            cast(on_vector, dst, w1_raw[u][:].rearrange("p j (m t) -> p m j t", t=PACK))
+        def cast_w1(a, z, on_vector):
+            dst = w1_bf[:].rearrange("p (t m j) -> p m j t", t=PACK, j=PACK)[:, a:z]
+            cast(on_vector, dst, w1_raw[:].rearrange("p j (m t) -> p m j t", t=PACK)[:, a:z])
 
         def cast_x(a, z, on_vector):
             c = a // CH
@@ -117,8 +116,8 @@ def tile_list_hscat_m_silu_kernel(tc, x, w1, w2_words, w2_scales, b, wgo, offs, 
                 out=h_codes[:, a:z].bitcast(FP8X4), scales=h_scales[:, a:z], in_=h_bf[:, PACK * a : PACK * z]
             )
 
-        def first_layer(c):
-            for a in range(c * CH, (c + 1) * CH, BLOCK):
+        def first_layer(start, stop):
+            for a in range(start, stop, BLOCK):
                 bank = banks[a // BLOCK % H_BANKS]
                 for t in range(PACK):
                     nc.tensor.matmul_mx(
@@ -156,29 +155,30 @@ def tile_list_hscat_m_silu_kernel(tc, x, w1, w2_words, w2_scales, b, wgo, offs, 
             for a in range(0, T, 2048):
                 nc.sync.dma_start(out=out[h * P : (h + 1) * P, a : a + 2048], in_=pages[h][:, a : a + 2048])
 
-        cast_w1(0, False)
-        cast_w1(1, True)
+        cast_w1(0, 56, False)
+        cast_w1(56, P, True)
         nc.vector.quantize_mx(out=w1_codes[:].bitcast(FP8X4), scales=w1_scales[:], in_=w1_bf[:])
         for a in (0, BLOCK):
             cast_x(a, a + BLOCK, False)
             quant_x(a, a + BLOCK)
-        first_layer(0)
-        quant_h(0, CH)
-        cast_x(CH, 2 * CH, True)
-        quant_x(CH, 2 * CH)
-        second_layer(0, 0, CH, banks[6], gated[0][:, 0:CH])
-        cast_x(2 * CH, 3 * CH, True)
-        quant_x(2 * CH, 3 * CH)
+        first_layer(0, BLOCK)
+        quant_h(0, BLOCK)
+        first_layer(BLOCK, CH)
+        second_layer(0, 0, BLOCK, banks[6], gated[0][:, 0:BLOCK])
+        quant_h(BLOCK, CH)
+        second_layer(0, BLOCK, CH, banks[5], gated[0][:, BLOCK:CH])
+        for c in (1, 2):
+            cast_x(c * CH, (c + 1) * CH, True)
+            quant_x(c * CH, (c + 1) * CH)
         scatter(0, 0, CH, gated[0][:, 0:CH])
-        first_layer(1)
+        first_layer(CH, 2 * CH)
         second_layer(1, 0, CH, banks[7], gated[1][:, 0:CH])
         quant_h(CH, 2 * CH)
         scatter(1, 0, CH, gated[1][:, 0:CH])
-        for k in range(1, 5):
-            ahead = range(k + 2, k + 3) if k < 4 else range(6, 8)
+        for k, ahead in ((1, range(3, 4)), (2, range(4, 6)), (3, range(6, 8))):
             for c in ahead:
                 cast_x(c * CH, (c + 1) * CH, False)
-            first_layer(k + 1)
+            first_layer((k + 1) * CH, (k + 2) * CH)
             quant_h((k + 1) * CH, (k + 2) * CH)
             quant_x(ahead.start * CH, ahead.stop * CH)
             spent = x_raw[ahead.stop - 1]
@@ -186,16 +186,16 @@ def tile_list_hscat_m_silu_kernel(tc, x, w1, w2_words, w2_scales, b, wgo, offs, 
                 second_layer(h, k * CH, (k + 1) * CH, banks[6 + h], spent[:, h, :])
             for h in range(2):
                 scatter(h, k * CH, (k + 1) * CH, spent[:, h, :])
-        first_layer(6)
-        first_layer(7)
-        quant_h(6 * CH, 8 * CH)
-        last = banks[15 % H_BANKS]
-        second_layer(0, 5 * CH, 6 * CH, last, gated[0][:, 5 * CH : 6 * CH])
-        scatter(0, 5 * CH, 6 * CH, gated[0][:, 5 * CH : 6 * CH])
-        second_layer(0, 6 * CH, S, banks[6], gated[0][:, 6 * CH : S])
-        second_layer(1, 5 * CH, 6 * CH, last, gated[1][:, 5 * CH : 6 * CH])
-        second_layer(1, 6 * CH, S, banks[7], gated[1][:, 6 * CH : S])
-        scatter(0, 6 * CH, S, gated[0][:, 6 * CH : S])
-        store(0)
-        scatter(1, 5 * CH, S, gated[1][:, 5 * CH : S])
-        store(1)
+        first_layer(5 * CH, 7 * CH)
+        quant_h(5 * CH, 7 * CH)
+        second_layer(0, 4 * CH, 5 * CH, banks[13 % H_BANKS], gated[0][:, 4 * CH : 5 * CH])
+        scatter(0, 4 * CH, 5 * CH, gated[0][:, 4 * CH : 5 * CH])
+        first_layer(7 * CH, S)
+        quant_h(7 * CH, S)
+        second_layer(1, 4 * CH, 5 * CH, banks[15 % H_BANKS], gated[1][:, 4 * CH : 5 * CH])
+        scatter(1, 4 * CH, 5 * CH, gated[1][:, 4 * CH : 5 * CH])
+        for h in range(2):
+            second_layer(h, 5 * CH, 7 * CH, banks[6], gated[h][:, 5 * CH : 7 * CH])
+            second_layer(h, 7 * CH, S, banks[7], gated[h][:, 7 * CH : S])
+            scatter(h, 5 * CH, S, gated[h][:, 5 * CH : S])
+            store(h)

from contextlib import ExitStack

import concourse.mybir as mybir

K, H, M, T, S = 512, 512, 256, 4096, 2048
FLOPS = 2 * K * H * S + 2 * H * M * S

F32 = mybir.dt.float32
BF16 = mybir.dt.bfloat16
I32 = mybir.dt.int32
U32 = mybir.dt.uint32
U16 = mybir.dt.uint16
U8 = mybir.dt.uint8
FP8X4 = mybir.dt.float8_e4m3fn_x4
FP4X4 = mybir.dt.float4_e2m1fn_x4
ACT = mybir.ActivationFunctionType
ALU = mybir.AluOpType

P = 128
PACK = 4
CH = 256
NCH = S // CH
BLOCK = 128
H_BANKS = 6


def tile_list_hscat_m_silu_kernel(tc, x, w1, w2_words, w2_scales, b, wgo, offs, out):
    nc = tc.nc
    with ExitStack() as ctx:
        keep = ctx.enter_context(tc.tile_pool(name="keep", bufs=1))
        psum = ctx.enter_context(tc.psum_pool(name="psum", bufs=1))

        offsets = keep.tile([P, S // 16], U16, name="offsets")
        pages = [keep.tile([P, T], F32, name="page%d" % h) for h in range(2)]
        gated = [keep.tile([P, S], F32, name="gated%d" % h) for h in range(2)]
        wgo_sb = keep.tile([P, S], F32, name="wgo_sb")
        bias = keep.tile([P, 2], F32, name="bias")
        zero = keep.tile([P, 1], F32, name="zero")
        relu_bias = keep.tile([P, 1], F32, name="relu_bias")
        w1_raw = keep.tile([P, PACK, H], F32, name="w1_raw")
        w1_bf = keep.tile([P, PACK * H], BF16, name="w1_bf", align_bytes=64)
        w1_codes = keep.tile([P, H], U32, name="w1_codes", align_bytes=64)
        w1_scales = keep.tile([P, H], U8, name="w1_scales", align_bytes=64)
        w2_codes = keep.tile([P, 2 * M], U8, name="w2_codes", align_bytes=64)
        w2_plane = keep.tile([P, M], U8, name="w2_plane", align_bytes=64)
        x_raw = [keep.tile([P, PACK, CH], F32, name="x_raw%d" % c) for c in range(NCH)]
        x_bf = keep.tile([P, PACK * S], BF16, name="x_bf", align_bytes=64)
        x_codes = keep.tile([P, S], U32, name="x_codes", align_bytes=64)
        x_scales = keep.tile([P, S], U8, name="x_scales", align_bytes=64)
        h_bf = keep.tile([P, PACK * S], BF16, name="h_bf", align_bytes=64)
        h_codes = keep.tile([P, S], U32, name="h_codes", align_bytes=64)
        h_scales = keep.tile([P, S], U8, name="h_scales", align_bytes=64)
        banks = [psum.tile([P, PACK * BLOCK], F32, name="bank%d" % i) for i in range(8)]

        x_view = x.rearrange("(p j) s -> p j s", j=PACK)
        w1_view = w1.rearrange("(p j) r -> p j r", j=PACK)

        def load_x(c):
            nc.sync.dma_start(out=x_raw[c][:], in_=x_view[:, :, c * CH : (c + 1) * CH])

        def load_wgo(a, z):
            nc.sync.dma_start(out=wgo_sb[:, a:z], in_=wgo[:, a:z])

        nc.gpsimd.memset(w2_plane[:].bitcast(I32), 0)
        nc.gpsimd.memset(zero[:], 0.0)
        for q in range(4):
            nc.scalar.dma_start(
                out=w2_plane[32 * q : 32 * q + 4, :].bitcast(I32),
                in_=w2_scales[0, 4 * q : 4 * q + 4, :].bitcast(I32),
            )
        nc.scalar.activation(out=relu_bias[:], in_=zero[:], func=ACT.Silu)

        nc.sync.dma_start(out=w1_raw[:], in_=w1_view)
        load_x(0)
        load_x(1)
        nc.sync.dma_start(out=w2_codes[:].bitcast(I32), in_=w2_words[0].bitcast(I32))
        load_x(2)
        with nc.allow_non_contiguous_dma(reason="one bias value to a partition"):
            nc.sync.dma_start(out=bias[:], in_=b.rearrange("(h p) -> p h", p=P))
        nc.sync.dma_start(offsets[:], offs)
        load_wgo(0, 512)
        load_x(3)
        load_x(4)
        load_wgo(512, 1024)
        load_x(5)
        load_x(6)
        load_wgo(1024, 2048)
        load_x(7)

        nc.vector.memset(pages[0][:, 0:2047], 0.0)
        nc.vector.memset(pages[0][:, 2047:T], 0.0)
        nc.gpsimd.memset(pages[1][:], 0.0)

        def cast(on_vector, dst, src):
            if on_vector:
                nc.vector.tensor_copy(out=dst, in_=src)
            else:
                nc.scalar.copy(out=dst, in_=src)

        def cast_w1(a, z, on_vector):
            dst = w1_bf[:].rearrange("p (t m j) -> p m j t", t=PACK, j=PACK)[:, a:z]
            cast(on_vector, dst, w1_raw[:].rearrange("p j (m t) -> p m j t", t=PACK)[:, a:z])

        def cast_x(a, z, on_vector):
            c = a // CH
            dst = x_bf[:, PACK * a : PACK * z].rearrange("p (g i j) -> p g j i", i=4, j=PACK)
            cast(on_vector, dst, x_raw[c][:, :, a - c * CH : z - c * CH].rearrange("p j (g i) -> p g j i", i=4))

        def quant_x(a, z):
            nc.vector.quantize_mx(
                out=x_codes[:, a:z].bitcast(FP8X4), scales=x_scales[:, a:z], in_=x_bf[:, PACK * a : PACK * z]
            )

        def quant_h(a, z):
            nc.vector.quantize_mx(
                out=h_codes[:, a:z].bitcast(FP8X4), scales=h_scales[:, a:z], in_=h_bf[:, PACK * a : PACK * z]
            )

        def first_layer(start, stop):
            for a in range(start, stop, BLOCK):
                bank = banks[a // BLOCK % H_BANKS]
                for t in range(PACK):
                    nc.tensor.matmul_mx(
                        out=bank[:, t * BLOCK : (t + 1) * BLOCK],
                        lhsT=w1_codes[:, t * P : (t + 1) * P].bitcast(FP8X4),
                        lhsT_scale=w1_scales[:, t * P : (t + 1) * P],
                        rhs=x_codes[:, a : a + BLOCK].bitcast(FP8X4),
                        rhs_scale=x_scales[:, a : a + BLOCK],
                        start=True,
                        stop=True,
                    )
                nc.scalar.activation(
                    out=h_bf[:, PACK * a : PACK * (a + BLOCK)].rearrange("p (n t) -> p n t", t=PACK),
                    in_=bank[:].rearrange("p (t n) -> p n t", t=PACK),
                    func=ACT.Relu,
                    bias=relu_bias[:],
                )

        def second_layer(h, a, z, bank, dst):
            nc.tensor.matmul_mx(
                out=bank[:, 0 : z - a],
                lhsT=w2_codes[:, 2 * P * h : 2 * P * (h + 1)].bitcast(FP4X4),
                lhsT_scale=w2_plane[:, P * h : P * (h + 1)],
                rhs=h_codes[:, a:z].bitcast(FP8X4),
                rhs_scale=h_scales[:, a:z],
                start=True,
                stop=True,
            )
            nc.scalar.activation(out=dst, in_=bank[:, 0 : z - a], func=ACT.Silu, bias=bias[:, h : h + 1])

        def scatter(h, a, z, src):
            nc.vector.tensor_tensor(pages[h][:].indirect(offsets[:, a // 16 : z // 16]), src, wgo_sb[:, a:z], ALU.mult)

        def store(h):
            for a in range(0, T, 2048):
                nc.sync.dma_start(out=out[h * P : (h + 1) * P, a : a + 2048], in_=pages[h][:, a : a + 2048])

        cast_w1(0, 56, False)
        cast_w1(56, P, True)
        nc.vector.quantize_mx(out=w1_codes[:].bitcast(FP8X4), scales=w1_scales[:], in_=w1_bf[:])
        for a in (0, BLOCK):
            cast_x(a, a + BLOCK, False)
            quant_x(a, a + BLOCK)
        first_layer(0, BLOCK)
        quant_h(0, BLOCK)
        first_layer(BLOCK, CH)
        second_layer(0, 0, BLOCK, banks[6], gated[0][:, 0:BLOCK])
        quant_h(BLOCK, CH)
        second_layer(0, BLOCK, CH, banks[5], gated[0][:, BLOCK:CH])
        for c in (1, 2):
            cast_x(c * CH, (c + 1) * CH, True)
            quant_x(c * CH, (c + 1) * CH)
        scatter(0, 0, CH, gated[0][:, 0:CH])
        first_layer(CH, 2 * CH)
        second_layer(1, 0, CH, banks[7], gated[1][:, 0:CH])
        quant_h(CH, 2 * CH)
        scatter(1, 0, CH, gated[1][:, 0:CH])
        for k, ahead in ((1, range(3, 4)), (2, range(4, 6)), (3, range(6, 8))):
            for c in ahead:
                cast_x(c * CH, (c + 1) * CH, False)
            first_layer((k + 1) * CH, (k + 2) * CH)
            quant_h((k + 1) * CH, (k + 2) * CH)
            quant_x(ahead.start * CH, ahead.stop * CH)
            spent = x_raw[ahead.stop - 1]
            for h in range(2):
                second_layer(h, k * CH, (k + 1) * CH, banks[6 + h], spent[:, h, :])
            for h in range(2):
                scatter(h, k * CH, (k + 1) * CH, spent[:, h, :])
        first_layer(5 * CH, 7 * CH)
        quant_h(5 * CH, 7 * CH)
        second_layer(0, 4 * CH, 5 * CH, banks[13 % H_BANKS], gated[0][:, 4 * CH : 5 * CH])
        scatter(0, 4 * CH, 5 * CH, gated[0][:, 4 * CH : 5 * CH])
        first_layer(7 * CH, S)
        quant_h(7 * CH, S)
        second_layer(1, 4 * CH, 5 * CH, banks[15 % H_BANKS], gated[1][:, 4 * CH : 5 * CH])
        scatter(1, 4 * CH, 5 * CH, gated[1][:, 4 * CH : 5 * CH])
        for h in range(2):
            second_layer(h, 5 * CH, 7 * CH, banks[6], gated[h][:, 5 * CH : 7 * CH])
            second_layer(h, 7 * CH, S, banks[7], gated[h][:, 7 * CH : S])
            scatter(h, 5 * CH, S, gated[h][:, 5 * CH : S])
            store(h)
